import numpy as np
import ml_dtypes


def mxq(x, axis, fmt="e4m3"):
    dtype, down = {"e4m3": (ml_dtypes.float8_e4m3fn, 7), "e5m2": (ml_dtypes.float8_e5m2, 14)}[fmt]
    v = np.moveaxis(np.asarray(x, np.float32).astype(ml_dtypes.bfloat16).astype(np.float64), axis, -1)
    blocks = v.reshape(v.shape[:-1] + (-1, 32))
    amax = np.abs(blocks).max(-1, keepdims=True)
    byte = np.maximum(np.where(amax > 0, np.frexp(amax)[1] - 1 + 127, 0) - down, 1)
    scale = np.exp2(byte - 127.0)
    codes = (blocks / scale).astype(np.float32).astype(dtype).astype(np.float64)
    return np.moveaxis((codes * scale).reshape(v.shape), -1, axis)


WIDE = False


def mx_kscale(k):
    if not WIDE:
        return np.ones(k)
    levels = np.array([10, -10, 5, -5, 0])
    if k % 512:
        return np.exp2(np.random.permutation(np.resize(levels, k // 32))).repeat(32)
    a = np.empty((k // 512, 16))
    for p in range(k // 512):
        a[p, :8] = np.random.permutation(np.resize(levels, 8))
        for g in range(8):
            far = levels[np.abs(levels - a[p, g]) >= 10]
            a[p, g + 8] = far[np.random.randint(len(far))]
    return np.exp2(a.ravel()).repeat(32)


def f64(x):
    return np.asarray(x).astype(np.float64)


def striped(idx):
    return np.tile(idx.reshape(-1, 16).T, (8, 1)).astype(np.uint16)


def unstriped(offs):
    return offs[:16].T.reshape(-1).astype(np.int64)


E2M1 = np.array([0.0, 0.5, 1.0, 1.5, 2.0, 3.0, 4.0, 6.0, -0.0, -0.5, -1.0, -1.5, -2.0, -3.0, -4.0, -6.0])


def pack_weight(w, fmt):
    k, n = w.shape
    w = f64(np.asarray(w, np.float32).astype(ml_dtypes.bfloat16)).reshape(k // 32, 32, n)
    amax = np.abs(w).max(1)
    if fmt == "e4m3":
        byte = np.frexp(amax)[1] - 1 + 127 - 7
    else:
        mant, ex = np.frexp(amax / 6.0)
        byte = np.where(mant > 0.5, ex, ex - 1) + 127
    byte = np.clip(np.where(amax > 0, byte, 1), 1, 254)
    scaled = (w * np.exp2(127.0 - byte)[:, None, :]).reshape(k, n).astype(np.float32)
    by_word = np.ascontiguousarray(scaled.reshape(k // 512, 128, 4, n).transpose(0, 1, 3, 2))
    if fmt == "e4m3":
        words = by_word.astype(ml_dtypes.float8_e4m3fn).view(np.uint8)
    else:
        c = by_word.astype(ml_dtypes.float4_e2m1fn).view(np.uint8) & 0xF
        words = (c[..., 0::2] | (c[..., 1::2] << 4)).reshape(k // 512, 128, 2 * n)
    return np.ascontiguousarray(words), np.ascontiguousarray(byte.astype(np.uint8).reshape(k // 512, 16, n))


def unpack_weight(words, scales, fmt):
    g, _, n = scales.shape
    words = np.ascontiguousarray(words).reshape(g, 128, n, -1)
    if fmt == "e4m3":
        vals = words.view(ml_dtypes.float8_e4m3fn).astype(np.float64)
    else:
        nib = np.empty((g, 128, n, 4), np.uint8)
        nib[..., 0::2] = words & 0xF
        nib[..., 1::2] = words >> 4
        vals = E2M1[nib]
    vals = vals * np.repeat(np.exp2(scales.astype(np.float64) - 127.0), 8, axis=1)[..., None]
    return vals.transpose(0, 1, 3, 2).reshape(g * 512, n)


def gelu(v):
    return 0.5 * v * (1.0 + np.tanh(np.sqrt(2.0 / np.pi) * (v + 0.044715 * v**3)))


K, H, T, S, T3, S2, P = 1024, 1024, 2048, 1024, 2048, 512, 512


def setup_inputs():
    n = np.random.standard_normal
    s = mx_kscale(K)[:, None]
    u = mx_kscale(H)[:, None]
    tab_words, tab_scales = pack_weight(n((K, T)) * s, "e4m3")
    tab2_words, tab2_scales = pack_weight(n((H, T3)) / u / np.sqrt(H), "e4m3")
    w4_words, w4_scales = pack_weight(n((H, H)) * u.T / u / np.sqrt(H), "e2m1")
    return {
        "tab_words": tab_words, "tab_scales": tab_scales,
        "offs": striped(np.random.permutation(T)[:S]),
        "tab2_words": tab2_words, "tab2_scales": tab2_scales,
        "offs2": striped(np.random.permutation(T3)[:S2]),
        "pos1": striped(np.random.permutation(S)[:P]),
        "pos2": striped(np.random.permutation(S)[:P]),
        "w1": (1.2 * n((K, H)) / s / np.sqrt(K)).astype(np.float32),
        "b1": (0.5 * n(H)).astype(np.float32),
        "gain": (np.random.uniform(0.7, 1.9, H) * u[:, 0]).astype(np.float32),
        "w4_words": w4_words, "w4_scales": w4_scales,
        "b2": (0.5 * n(H) * u[:, 0]).astype(np.float32),
        "tol": n(S2).astype(np.float32),
        "lean": (0.3 * n((S2, P))).astype(np.float32),
    }


def reference(tab_words, tab_scales, offs, tab2_words, tab2_scales, offs2, pos1, pos2,
              w1, b1, gain, w4_words, w4_scales, b2, tol, lean):
    v = unpack_weight(tab_words, tab_scales, "e4m3")[:, unstriped(offs)]
    v2 = unpack_weight(tab2_words, tab2_scales, "e4m3")[:, unstriped(offs2)]
    w4 = unpack_weight(w4_words, w4_scales, "e2m1")
    x = mxq(f64(w1), 0, "e4m3").T @ v
    h = np.tanh(x + f64(b1)[:, None]) * f64(gain)[:, None]
    hq = mxq(h, 0, "e4m3")
    f = (w4.T @ hq) + f64(b2)[:, None]
    fq = mxq(f, 0, "e4m3")
    e = v2.T @ hq
    d = v2.T @ fq
    a = 1.0 / (1.0 + np.exp(-(e[:, unstriped(pos1)] + f64(tol)[:, None])))
    return a * d[:, unstriped(pos2)] + f64(lean)

@@ -1,0 +1,278 @@
+from contextlib import ExitStack
+
+import concourse.mybir as mybir
+
+K, H, T, S, S2, NP = 1024, 1024, 2048, 1024, 512, 512
+FLOPS = 2 * (K * H * S + H * H * S + 2 * H * S2 * S)
+
+F32 = mybir.dt.float32
+BF16 = mybir.dt.bfloat16
+I32 = mybir.dt.int32
+U32 = mybir.dt.uint32
+U16 = mybir.dt.uint16
+U8 = mybir.dt.uint8
+FP8X4 = mybir.dt.float8_e4m3fn_x4
+FP4X4 = mybir.dt.float4_e2m1fn_x4
+ACT = mybir.ActivationFunctionType
+ALU = mybir.AluOpType
+
+P = 128
+PACK = 4
+KP = P * PACK
+PASSES = 2
+CH = 512
+CHUNKS = S // CH
+MT = S2 // P
+
+
+def tile_list_guide_cut_tolerance_kernel(
+    tc, tab_words, tab_scales, offs, tab2_words, tab2_scales, offs2, pos1, pos2,
+    w1, b1, gain, w4_words, w4_scales, b2, tol, lean, out,
+):
+    nc = tc.nc
+    with ExitStack() as ctx:
+        keep = ctx.enter_context(tc.tile_pool(name="keep", bufs=1))
+        ring = ctx.enter_context(tc.tile_pool(name="ring", bufs=2))
+        psum = ctx.enter_context(tc.psum_pool(name="psum", bufs=8))
+
+        def held(name, shape, dtype):
+            return keep.tile(shape, dtype, name=name, align_bytes=64)
+
+        def load_list(name, src):
+            dst = held(name, list(src.shape), U16)
+            nc.sync.dma_start(dst[:], src)
+            return dst
+
+        def load_words(name, src):
+            dst = held(name, [P, T], I32)
+            nc.sync.dma_start(dst[:], src.rearrange("p t i -> p (t i)").bitcast(I32))
+            return dst
+
+        def load_table_scales(dst, src):
+            for q in range(4):
+                nc.sync.dma_start(dst[32 * q : 32 * q + 4 * PASSES, :].bitcast(I32), src[:, 4 * q : 4 * q + 4, :].bitcast(I32))
+
+        def load_w1(a, b):
+            dst = held("w1_raw%d%d" % (a, b), [P, PACK, KP], F32)
+            nc.sync.dma_start(dst[:], w1[a * KP : (a + 1) * KP, b * KP : (b + 1) * KP].rearrange("(p j) c -> p j c", j=PACK))
+            return dst
+
+        def load_channel_vector(name, src):
+            dst = held(name, [P, PASSES * PACK], F32)
+            nc.sync.dma_start(dst[:].rearrange("p (b t) -> p b t", t=PACK), src.rearrange("(b p t) -> p b t", p=P, t=PACK))
+            return dst
+
+        tab_sc = held("tab_sc", [P, T], U8)
+        tab2_sc = held("tab2_sc", [P, T], U8)
+        w4_sc_raw = held("w4_sc_raw", [P, PASSES * H], U8)
+        nc.gpsimd.memset(tab_sc[:, : T // 2].bitcast(I32), 0)
+        nc.vector.memset(tab_sc[:, T // 2 :].bitcast(I32), 0)
+        nc.gpsimd.memset(tab2_sc[:].bitcast(I32), 0)
+        nc.gpsimd.memset(w4_sc_raw[:].bitcast(I32), 0)
+
+        w1_raw = {}
+        offs_sb = load_list("offs_sb", offs)
+        offs2_sb = load_list("offs2_sb", offs2)
+        load_table_scales(tab_sc, tab_scales)
+        w1_raw[0, 0] = load_w1(0, 0)
+        load_table_scales(tab2_sc, tab2_scales)
+        tab_w = [load_words("tab_w0", tab_words[0])]
+        for q in range(4):
+            nc.sync.dma_start(
+                w4_sc_raw[32 * q : 32 * q + 4, :].bitcast(I32).rearrange("r (a n) -> r a n", a=PASSES),
+                w4_scales[:, 4 * q : 4 * q + 4, :].bitcast(I32).rearrange("a r n -> r a n"),
+            )
+        w1_raw[1, 0] = load_w1(1, 0)
+        tab_w.append(load_words("tab_w1", tab_words[1]))
+        w1_raw[0, 1] = load_w1(0, 1)
+        b1_sb = load_channel_vector("b1_sb", b1)
+        gain_sb = load_channel_vector("gain_sb", gain)
+        w1_raw[1, 1] = load_w1(1, 1)
+        w4_raw = held("w4_raw", [P, PASSES * H // 2], I32)
+        nc.sync.dma_start(w4_raw[:].rearrange("p (a n) -> p a n", a=PASSES), w4_words.bitcast(I32).rearrange("a p n -> p a n"))
+        tab2_w = [load_words("tab2_w0", tab2_words[0])]
+        b2_sb = load_channel_vector("b2_sb", b2)
+        tab2_w.append(load_words("tab2_w1", tab2_words[1]))
+        pos1_sb = load_list("pos1_sb", pos1)
+        pos2_sb = load_list("pos2_sb", pos2)
+        tol_sb = held("tol_sb", [P, MT], F32)
+        with nc.allow_non_contiguous_dma(reason="one tolerance for each partition and row tile"):
+            nc.sync.dma_start(tol_sb[:], tol.rearrange("(i p) -> p i", p=P))
+        lean_sb = held("lean_sb", [P, MT, NP], F32)
+        nc.sync.dma_start(lean_sb[:], lean.rearrange("(i p) n -> p i n", p=P))
+
+        def gather(name, window, offsets, count, dtype):
+            dst = held(name, [P, count], dtype)
+            nc.vector.tensor_copy(dst[:], window.indirect(offsets))
+            return dst
+
+        def quantize(name, grouped):
+            codes = held(name + "_codes", [P, KP], U32)
+            scales = held(name + "_scales", [P, KP], U8)
+            nc.vector.quantize_mx(out=codes[:].bitcast(FP8X4), scales=scales[:], in_=grouped[:])
+            return codes, scales
+
+        def grouped_tile():
+            return ring.tile([P, KP * PACK], BF16, name="grouped", bufs=3, align_bytes=64)
+
+        def round_w1(a, b, scalar_share):
+            grouped = grouped_tile()
+            src = w1_raw[a, b][:].rearrange("p j (m t) -> p m j t", t=PACK)
+            dst = grouped[:].rearrange("p (t m j) -> p m j t", t=PACK, j=PACK)
+            if scalar_share > 0:
+                nc.scalar.copy(dst[:, :scalar_share], src[:, :scalar_share])
+            if scalar_share < P:
+                nc.vector.tensor_copy(dst[:, scalar_share:], src[:, scalar_share:])
+            return grouped
+
+        def bank():
+            return psum.tile([P, CH], F32, name="bank")
+
+        v_sc = gather("v_sc", tab_sc[:], offs_sb[:], S, U8)
+        v_w = {}
+
+        def gather_sites(a, c):
+            v_w[a, c] = gather("v_w%d%d" % (a, c), tab_w[a][:].bitcast(U32), offs_sb[:, c * CH // 16 : (c + 1) * CH // 16], CH, U32)
+
+        w1q, hq, fq = {}, {}, {}
+
+        def first_pass(acc, a, b, c, t):
+            codes, scales = w1q[a, b]
+            cols = slice(c * CH, (c + 1) * CH)
+            nc.tensor.matmul_mx(
+                out=acc[:], lhsT=codes[:, t * P : (t + 1) * P].bitcast(FP8X4), lhsT_scale=scales[:, t * P : (t + 1) * P],
+                rhs=v_w[a, c][:].bitcast(FP8X4), rhs_scale=v_sc[4 * a :, cols], start=(a == 0), stop=(a == PASSES - 1),
+            )
+
+        def tanh_unit(b, accs):
+            th = ring.tile([P, PACK, CH], F32, name="th", bufs=3)
+            for t in range(PACK):
+                nc.scalar.activation(th[:, t, :], accs[t][:], ACT.Tanh, bias=b1_sb[:, PACK * b + t : PACK * b + t + 1])
+            return th
+
+        def gain_unit(b, th):
+            grouped = grouped_tile()
+            factor = gain_sb[:, PACK * b : PACK * (b + 1)].unsqueeze(1).unsqueeze(3).to_broadcast([P, CH // 4, PACK, 4])
+            nc.vector.tensor_tensor(
+                grouped[:].rearrange("p (g i t) -> p g t i", i=4, t=PACK),
+                th[:].rearrange("p t (g i) -> p g t i", i=4), factor, ALU.mult,
+            )
+            return grouped
+
+        def first_level(b, c):
+            accs = [bank() for t in range(PACK)]
+            for t in range(PACK):
+                for a in range(PASSES):
+                    first_pass(accs[t], a, b, c, t)
+            return tanh_unit(b, accs)
+
+        w1q[0, 0] = quantize("w1q00", round_w1(0, 0, P))
+        head = [[bank() for t in range(PACK)] for c in range(CHUNKS)]
+        for c in range(CHUNKS):
+            gather_sites(0, c)
+            for t in range(PACK):
+                first_pass(head[c][t], 0, 0, c, t)
+        gather_sites(1, 0)
+        w1q[1, 0] = quantize("w1q10", round_w1(1, 0, P))
+        for t in range(PACK):
+            first_pass(head[0][t], 1, 0, 0, t)
+        gather_sites(1, 1)
+        for t in range(PACK):
+            first_pass(head[1][t], 1, 0, 1, t)
+        v2_sc = gather("v2_sc", tab2_sc[:], offs2_sb[:], S2, U8)
+        w4_sc = held("w4_sc", [P, PASSES * H], U8)
+        nc.vector.tensor_copy(
+            w4_sc[:].rearrange("p (g t m) -> p g t m", t=PACK, m=P), w4_sc_raw[:].rearrange("p (g m t) -> p g t m", t=PACK, m=P)
+        )
+        th00 = tanh_unit(0, head[0])
+        w1q[0, 1] = quantize("w1q01", round_w1(0, 1, 0))
+        w1q[1, 1] = quantize("w1q11", round_w1(1, 1, 0))
+        hq[0, 0] = quantize("hq00", gain_unit(0, th00))
+        th10 = first_level(1, 0)
+        hq[1, 0] = quantize("hq10", gain_unit(1, th10))
+        th01 = tanh_unit(0, head[1])
+        w4_w = held("w4_w", [P, PASSES * H], U16)
+        nc.scalar.copy(
+            w4_w[:].rearrange("p (g t m) -> p g t m", t=PACK, m=P),
+            w4_raw[:].bitcast(U16).rearrange("p (g m t) -> p g t m", t=PACK, m=P),
+        )
+        v2_w = [gather("v2_w%d" % a, tab2_w[a][:].bitcast(U32), offs2_sb[:], S2, U32) for a in range(PASSES)]
+        th11 = first_level(1, 1)
+        hq[0, 1] = quantize("hq01", gain_unit(0, th01))
+        hq[1, 1] = quantize("hq11", gain_unit(1, th11))
+
+        w4_bytes = w4_w[:].bitcast(U8)
+
+        def second_level(b, c):
+            grouped = grouped_tile()
+            shift = b2_sb[:, PACK * b : PACK * (b + 1)].unsqueeze(1).to_broadcast([P, P, PACK])
+            for q in range(CH // P):
+                acc = bank()
+                cols = slice(q * P, (q + 1) * P)
+                for t in range(PACK):
+                    for a in range(PASSES):
+                        first = a * H + b * KP + t * P
+                        codes, scales = hq[a, c]
+                        nc.tensor.matmul_mx(
+                            out=acc[:, t * P : (t + 1) * P],
+                            lhsT=w4_bytes[:, 2 * first : 2 * (first + P)].bitcast(FP4X4), lhsT_scale=w4_sc[:, first : first + P],
+                            rhs=codes[:, cols].bitcast(FP8X4), rhs_scale=scales[:, cols], start=(a == 0), stop=(a == PASSES - 1),
+                        )
+                nc.vector.tensor_tensor(
+                    grouped[:, q * KP : (q + 1) * KP].rearrange("p (n t) -> p n t", t=PACK),
+                    acc[:].rearrange("p (t n) -> p n t", t=PACK), shift, ALU.add,
+                )
+            return grouped
+
+        def second_level_wide(b, c):
+            planes = ring.tile([P, PACK, CH], BF16, name="planes")
+            for t in range(PACK):
+                acc = bank()
+                for a in range(PASSES):
+                    first = a * H + b * KP + t * P
+                    codes, scales = hq[a, c]
+                    nc.tensor.matmul_mx(
+                        out=acc[:], lhsT=w4_bytes[:, 2 * first : 2 * (first + P)].bitcast(FP4X4), lhsT_scale=w4_sc[:, first : first + P],
+                        rhs=codes[:].bitcast(FP8X4), rhs_scale=scales[:], start=(a == 0), stop=(a == PASSES - 1),
+                    )
+                nc.scalar.activation(planes[:, t, :], acc[:], ACT.Identity, bias=b2_sb[:, PACK * b + t : PACK * b + t + 1])
+            grouped = grouped_tile()
+            nc.vector.tensor_copy(
+                grouped[:].rearrange("p (g i t) -> p g t i", i=4, t=PACK), planes[:].rearrange("p t (g i) -> p g t i", i=4)
+            )
+            return grouped
+
+        e_sb = [held("e_sb%d" % i, [P, S], F32) for i in range(MT)]
+        d_sb = [held("d_sb%d" % i, [P, S], F32) for i in range(MT)]
+
+        def scores(dst, level, i, c):
+            acc = bank()
+            rows = slice(i * P, (i + 1) * P)
+            for a in range(PASSES):
+                codes, scales = level[a, c]
+                nc.tensor.matmul_mx(
+                    out=acc[:], lhsT=v2_w[a][:, rows].bitcast(FP8X4), lhsT_scale=v2_sc[4 * a :, rows],
+                    rhs=codes[:].bitcast(FP8X4), rhs_scale=scales[:], start=(a == 0), stop=(a == PASSES - 1),
+                )
+            nc.scalar.copy(dst[i][:, c * CH : (c + 1) * CH], acc[:])
+
+        for b in range(PASSES):
+            fq[b, 0] = quantize("fq%d0" % b, second_level_wide(b, 0))
+        for c in range(CHUNKS):
+            for i in range(MT):
+                scores(e_sb, hq, i, c)
+        for b in range(PASSES):
+            fq[b, 1] = quantize("fq%d1" % b, second_level(b, 1))
+        cut = []
+        for i in range(MT):
+            look = held("cut%d" % i, [P, NP], F32)
+            nc.scalar.activation(look[:], e_sb[i][:].indirect(pos1_sb[:]), ACT.Sigmoid, bias=tol_sb[:, i : i + 1])
+            cut.append(look)
+        for i in range(MT):
+            for c in range(CHUNKS):
+                scores(d_sb, fq, i, c)
+        for i in range(MT):
+            res = held("res%d" % i, [P, NP], F32)
+            nc.vector.tensor_tensor(res[:], d_sb[i][:].indirect(pos2_sb[:]), cut[i][:], ALU.mult)
+            nc.vector.tensor_tensor(res[:], res[:], lean_sb[:, i, :], ALU.add)
+            nc.sync.dma_start(out[i * P : (i + 1) * P, :], res[:])

@@ -67,15 +67,14 @@ def tile_list_guide_cut_tolerance_kernel(
         w4_sc_raw = held("w4_sc_raw", [P, PASSES * H], U8)
         nc.gpsimd.memset(tab_sc[:, : T // 2].bitcast(I32), 0)
         nc.vector.memset(tab_sc[:, T // 2 :].bitcast(I32), 0)
+        nc.vector.memset(w4_sc_raw[:].bitcast(I32), 0)
         nc.gpsimd.memset(tab2_sc[:].bitcast(I32), 0)
-        nc.gpsimd.memset(w4_sc_raw[:].bitcast(I32), 0)
 
         w1_raw = {}
         offs_sb = load_list("offs_sb", offs)
         offs2_sb = load_list("offs2_sb", offs2)
         load_table_scales(tab_sc, tab_scales)
         w1_raw[0, 0] = load_w1(0, 0)
-        load_table_scales(tab2_sc, tab2_scales)
         tab_w = [load_words("tab_w0", tab_words[0])]
         for q in range(4):
             nc.sync.dma_start(
@@ -91,8 +90,9 @@ def tile_list_guide_cut_tolerance_kernel(
         w4_raw = held("w4_raw", [P, PASSES * H // 2], I32)
         nc.sync.dma_start(w4_raw[:].rearrange("p (a n) -> p a n", a=PASSES), w4_words.bitcast(I32).rearrange("a p n -> p a n"))
         tab2_w = [load_words("tab2_w0", tab2_words[0])]
-        b2_sb = load_channel_vector("b2_sb", b2)
+        load_table_scales(tab2_sc, tab2_scales)
         tab2_w.append(load_words("tab2_w1", tab2_words[1]))
+        b2_sb = load_channel_vector("b2_sb", b2)
         pos1_sb = load_list("pos1_sb", pos1)
         pos2_sb = load_list("pos2_sb", pos2)
         tol_sb = held("tol_sb", [P, MT], F32)
@@ -109,20 +109,22 @@ def tile_list_guide_cut_tolerance_kernel(
         def quantize(name, grouped):
             codes = held(name + "_codes", [P, KP], U32)
             scales = held(name + "_scales", [P, KP], U8)
-            nc.vector.quantize_mx(out=codes[:].bitcast(FP8X4), scales=scales[:], in_=grouped[:])
+            for half in range(2):
+                cols = slice(half * KP // 2, (half + 1) * KP // 2)
+                nc.vector.quantize_mx(
+                    out=codes[:, cols].bitcast(FP8X4), scales=scales[:, cols], in_=grouped[:, PACK * cols.start : PACK * cols.stop]
+                )
             return codes, scales
 
         def grouped_tile():
             return ring.tile([P, KP * PACK], BF16, name="grouped", bufs=3, align_bytes=64)
 
-        def round_w1(a, b, scalar_share):
+        def round_w1(a, b, copy):
             grouped = grouped_tile()
             src = w1_raw[a, b][:].rearrange("p j (m t) -> p m j t", t=PACK)
             dst = grouped[:].rearrange("p (t m j) -> p m j t", t=PACK, j=PACK)
-            if scalar_share > 0:
-                nc.scalar.copy(dst[:, :scalar_share], src[:, :scalar_share])
-            if scalar_share < P:
-                nc.vector.tensor_copy(dst[:, scalar_share:], src[:, scalar_share:])
+            for half in range(2):
+                copy(dst[:, :, :, 2 * half : 2 * half + 2], src[:, :, :, 2 * half : 2 * half + 2])
             return grouped
 
         def bank():
@@ -152,11 +154,12 @@ def tile_list_guide_cut_tolerance_kernel(
 
         def gain_unit(b, th):
             grouped = grouped_tile()
-            factor = gain_sb[:, PACK * b : PACK * (b + 1)].unsqueeze(1).unsqueeze(3).to_broadcast([P, CH // 4, PACK, 4])
-            nc.vector.tensor_tensor(
-                grouped[:].rearrange("p (g i t) -> p g t i", i=4, t=PACK),
-                th[:].rearrange("p t (g i) -> p g t i", i=4), factor, ALU.mult,
-            )
+            factor = gain_sb[:, PACK * b : PACK * (b + 1)].unsqueeze(1).unsqueeze(3).to_broadcast([P, CH // 8, PACK, 4])
+            dst = grouped[:].rearrange("p (g i t) -> p g t i", i=4, t=PACK)
+            src = th[:].rearrange("p t (g i) -> p g t i", i=4)
+            for half in range(2):
+                groups = slice(half * CH // 8, (half + 1) * CH // 8)
+                nc.vector.tensor_tensor(dst[:, groups], src[:, groups], factor, ALU.mult)
             return grouped
 
         def first_level(b, c):
@@ -166,27 +169,26 @@ def tile_list_guide_cut_tolerance_kernel(
                     first_pass(accs[t], a, b, c, t)
             return tanh_unit(b, accs)
 
-        w1q[0, 0] = quantize("w1q00", round_w1(0, 0, P))
+        w1q[0, 0] = quantize("w1q00", round_w1(0, 0, nc.scalar.copy))
         head = [[bank() for t in range(PACK)] for c in range(CHUNKS)]
         for c in range(CHUNKS):
             gather_sites(0, c)
             for t in range(PACK):
                 first_pass(head[c][t], 0, 0, c, t)
         gather_sites(1, 0)
-        w1q[1, 0] = quantize("w1q10", round_w1(1, 0, P))
+        w1q[1, 0] = quantize("w1q10", round_w1(1, 0, nc.scalar.copy))
         for t in range(PACK):
             first_pass(head[0][t], 1, 0, 0, t)
         gather_sites(1, 1)
         for t in range(PACK):
             first_pass(head[1][t], 1, 0, 1, t)
-        v2_sc = gather("v2_sc", tab2_sc[:], offs2_sb[:], S2, U8)
         w4_sc = held("w4_sc", [P, PASSES * H], U8)
         nc.vector.tensor_copy(
             w4_sc[:].rearrange("p (g t m) -> p g t m", t=PACK, m=P), w4_sc_raw[:].rearrange("p (g m t) -> p g t m", t=PACK, m=P)
         )
         th00 = tanh_unit(0, head[0])
-        w1q[0, 1] = quantize("w1q01", round_w1(0, 1, 0))
-        w1q[1, 1] = quantize("w1q11", round_w1(1, 1, 0))
+        w1q[0, 1] = quantize("w1q01", round_w1(0, 1, nc.vector.tensor_copy))
+        w1q[1, 1] = quantize("w1q11", round_w1(1, 1, nc.vector.tensor_copy))
         hq[0, 0] = quantize("hq00", gain_unit(0, th00))
         th10 = first_level(1, 0)
         hq[1, 0] = quantize("hq10", gain_unit(1, th10))
@@ -197,6 +199,7 @@ def tile_list_guide_cut_tolerance_kernel(
             w4_raw[:].bitcast(U16).rearrange("p (g m t) -> p g t m", t=PACK, m=P),
         )
         v2_w = [gather("v2_w%d" % a, tab2_w[a][:].bitcast(U32), offs2_sb[:], S2, U32) for a in range(PASSES)]
+        v2_sc = gather("v2_sc", tab2_sc[:], offs2_sb[:], S2, U8)
         th11 = first_level(1, 1)
         hq[0, 1] = quantize("hq01", gain_unit(0, th01))
         hq[1, 1] = quantize("hq11", gain_unit(1, th11))
@@ -237,9 +240,11 @@ def tile_list_guide_cut_tolerance_kernel(
                     )
                 nc.scalar.activation(planes[:, t, :], acc[:], ACT.Identity, bias=b2_sb[:, PACK * b + t : PACK * b + t + 1])
             grouped = grouped_tile()
-            nc.vector.tensor_copy(
-                grouped[:].rearrange("p (g i t) -> p g t i", i=4, t=PACK), planes[:].rearrange("p t (g i) -> p g t i", i=4)
-            )
+            dst = grouped[:].rearrange("p (g i t) -> p g t i", i=4, t=PACK)
+            src = planes[:].rearrange("p t (g i) -> p g t i", i=4)
+            for half in range(2):
+                groups = slice(half * CH // 8, (half + 1) * CH // 8)
+                nc.vector.tensor_copy(dst[:, groups], src[:, groups])
             return grouped
 
         e_sb = [held("e_sb%d" % i, [P, S], F32) for i in range(MT)]
@@ -271,8 +276,10 @@ def tile_list_guide_cut_tolerance_kernel(
         for i in range(MT):
             for c in range(CHUNKS):
                 scores(d_sb, fq, i, c)
-        for i in range(MT):
-            res = held("res%d" % i, [P, NP], F32)
-            nc.vector.tensor_tensor(res[:], d_sb[i][:].indirect(pos2_sb[:]), cut[i][:], ALU.mult)
-            nc.vector.tensor_tensor(res[:], res[:], lean_sb[:, i, :], ALU.add)
-            nc.sync.dma_start(out[i * P : (i + 1) * P, :], res[:])
+        res = [held("res%d" % i, [P, NP], F32) for i in range(MT)]
+        for i in range(MT + 1):
+            if i < MT:
+                nc.vector.tensor_tensor(res[i][:], d_sb[i][:].indirect(pos2_sb[:]), cut[i][:], ALU.mult)
+            if i > 0:
+                nc.vector.tensor_tensor(res[i - 1][:], res[i - 1][:], lean_sb[:, i - 1, :], ALU.add)
+                nc.sync.dma_start(out[(i - 1) * P : i * P, :], res[i - 1][:])

@@ -71,27 +71,28 @@ def tile_list_guide_cut_tolerance_kernel(
         nc.gpsimd.memset(tab2_sc[:].bitcast(I32), 0)
 
         w1_raw = {}
+        tab_w, tab2_w = {}, {}
         offs_sb = load_list("offs_sb", offs)
-        offs2_sb = load_list("offs2_sb", offs2)
+        b1_sb = load_channel_vector("b1_sb", b1)
         load_table_scales(tab_sc, tab_scales)
+        tab_w[0] = load_words("tab_w0", tab_words[0])
         w1_raw[0, 0] = load_w1(0, 0)
-        tab_w = [load_words("tab_w0", tab_words[0])]
         for q in range(4):
             nc.sync.dma_start(
                 w4_sc_raw[32 * q : 32 * q + 4, :].bitcast(I32).rearrange("r (a n) -> r a n", a=PASSES),
                 w4_scales[:, 4 * q : 4 * q + 4, :].bitcast(I32).rearrange("a r n -> r a n"),
             )
+        tab_w[1] = load_words("tab_w1", tab_words[1])
         w1_raw[1, 0] = load_w1(1, 0)
-        tab_w.append(load_words("tab_w1", tab_words[1]))
         w1_raw[0, 1] = load_w1(0, 1)
-        b1_sb = load_channel_vector("b1_sb", b1)
-        gain_sb = load_channel_vector("gain_sb", gain)
         w1_raw[1, 1] = load_w1(1, 1)
+        gain_sb = load_channel_vector("gain_sb", gain)
         w4_raw = held("w4_raw", [P, PASSES * H // 2], I32)
         nc.sync.dma_start(w4_raw[:].rearrange("p (a n) -> p a n", a=PASSES), w4_words.bitcast(I32).rearrange("a p n -> p a n"))
-        tab2_w = [load_words("tab2_w0", tab2_words[0])]
+        offs2_sb = load_list("offs2_sb", offs2)
+        tab2_w[0] = load_words("tab2_w0", tab2_words[0])
         load_table_scales(tab2_sc, tab2_scales)
-        tab2_w.append(load_words("tab2_w1", tab2_words[1]))
+        tab2_w[1] = load_words("tab2_w1", tab2_words[1])
         b2_sb = load_channel_vector("b2_sb", b2)
         pos1_sb = load_list("pos1_sb", pos1)
         pos2_sb = load_list("pos2_sb", pos2)
@@ -119,13 +120,15 @@ def tile_list_guide_cut_tolerance_kernel(
         def grouped_tile():
             return ring.tile([P, KP * PACK], BF16, name="grouped", bufs=3, align_bytes=64)
 
-        def round_w1(a, b, copy):
+        def round_w1(a, b, copies):
             grouped = grouped_tile()
             src = w1_raw[a, b][:].rearrange("p j (m t) -> p m j t", t=PACK)
             dst = grouped[:].rearrange("p (t m j) -> p m j t", t=PACK, j=PACK)
-            for half in range(2):
+            for half, copy in enumerate(copies):
                 copy(dst[:, :, :, 2 * half : 2 * half + 2], src[:, :, :, 2 * half : 2 * half + 2])
             return grouped
+
+        on_scalar, on_vector = nc.scalar.copy, nc.vector.tensor_copy
 
         def bank():
             return psum.tile([P, CH], F32, name="bank")
@@ -169,35 +172,35 @@ def tile_list_guide_cut_tolerance_kernel(
                     first_pass(accs[t], a, b, c, t)
             return tanh_unit(b, accs)
 
-        w1q[0, 0] = quantize("w1q00", round_w1(0, 0, nc.scalar.copy))
+        for a in range(PASSES):
+            for c in range(CHUNKS):
+                gather_sites(a, c)
+        w1q[0, 0] = quantize("w1q00", round_w1(0, 0, (on_scalar, on_scalar)))
         head = [[bank() for t in range(PACK)] for c in range(CHUNKS)]
         for c in range(CHUNKS):
-            gather_sites(0, c)
             for t in range(PACK):
                 first_pass(head[c][t], 0, 0, c, t)
-        gather_sites(1, 0)
-        w1q[1, 0] = quantize("w1q10", round_w1(1, 0, nc.scalar.copy))
-        for t in range(PACK):
-            first_pass(head[0][t], 1, 0, 0, t)
-        gather_sites(1, 1)
-        for t in range(PACK):
-            first_pass(head[1][t], 1, 0, 1, t)
+        w1q[1, 0] = quantize("w1q10", round_w1(1, 0, (on_vector, on_scalar)))
+        for c in range(CHUNKS):
+            for t in range(PACK):
+                first_pass(head[c][t], 1, 0, c, t)
         w4_sc = held("w4_sc", [P, PASSES * H], U8)
         nc.vector.tensor_copy(
             w4_sc[:].rearrange("p (g t m) -> p g t m", t=PACK, m=P), w4_sc_raw[:].rearrange("p (g m t) -> p g t m", t=PACK, m=P)
         )
         th00 = tanh_unit(0, head[0])
-        w1q[0, 1] = quantize("w1q01", round_w1(0, 1, nc.vector.tensor_copy))
-        w1q[1, 1] = quantize("w1q11", round_w1(1, 1, nc.vector.tensor_copy))
+        w1q[0, 1] = quantize("w1q01", round_w1(0, 1, (on_vector, on_vector)))
+        w1q[1, 1] = quantize("w1q11", round_w1(1, 1, (on_vector, on_scalar)))
         hq[0, 0] = quantize("hq00", gain_unit(0, th00))
         th10 = first_level(1, 0)
         hq[1, 0] = quantize("hq10", gain_unit(1, th10))
         th01 = tanh_unit(0, head[1])
         w4_w = held("w4_w", [P, PASSES * H], U16)
-        nc.scalar.copy(
-            w4_w[:].rearrange("p (g t m) -> p g t m", t=PACK, m=P),
-            w4_raw[:].bitcast(U16).rearrange("p (g m t) -> p g t m", t=PACK, m=P),
-        )
+        for g in (0, 2, 1, 3):
+            nc.scalar.copy(
+                w4_w[:, g * KP : (g + 1) * KP].rearrange("p (t m) -> p t m", t=PACK),
+                w4_raw[:].bitcast(U16)[:, g * KP : (g + 1) * KP].rearrange("p (m t) -> p t m", t=PACK),
+            )
         v2_w = [gather("v2_w%d" % a, tab2_w[a][:].bitcast(U32), offs2_sb[:], S2, U32) for a in range(PASSES)]
         v2_sc = gather("v2_sc", tab2_sc[:], offs2_sb[:], S2, U8)
         th11 = first_level(1, 1)
@@ -250,7 +253,7 @@ def tile_list_guide_cut_tolerance_kernel(
         e_sb = [held("e_sb%d" % i, [P, S], F32) for i in range(MT)]
         d_sb = [held("d_sb%d" % i, [P, S], F32) for i in range(MT)]
 
-        def scores(dst, level, i, c):
+        def scores(dst, level, i, c, copy=on_scalar):
             acc = bank()
             rows = slice(i * P, (i + 1) * P)
             for a in range(PASSES):
@@ -259,27 +262,24 @@ def tile_list_guide_cut_tolerance_kernel(
                     out=acc[:], lhsT=v2_w[a][:, rows].bitcast(FP8X4), lhsT_scale=v2_sc[4 * a :, rows],
                     rhs=codes[:].bitcast(FP8X4), rhs_scale=scales[:], start=(a == 0), stop=(a == PASSES - 1),
                 )
-            nc.scalar.copy(dst[i][:, c * CH : (c + 1) * CH], acc[:])
+            copy(dst[i][:, c * CH : (c + 1) * CH], acc[:])
 
         for b in range(PASSES):
             fq[b, 0] = quantize("fq%d0" % b, second_level_wide(b, 0))
-        for c in range(CHUNKS):
-            for i in range(MT):
-                scores(e_sb, hq, i, c)
-        for b in range(PASSES):
-            fq[b, 1] = quantize("fq%d1" % b, second_level(b, 1))
-        cut = []
         for i in range(MT):
-            look = held("cut%d" % i, [P, NP], F32)
-            nc.scalar.activation(look[:], e_sb[i][:].indirect(pos1_sb[:]), ACT.Sigmoid, bias=tol_sb[:, i : i + 1])
-            cut.append(look)
+            scores(e_sb, hq, i, 0)
+        fq[0, 1] = quantize("fq01", second_level(0, 1))
         for i in range(MT):
-            for c in range(CHUNKS):
-                scores(d_sb, fq, i, c)
+            scores(e_sb, hq, i, 1)
+        fq[1, 1] = quantize("fq11", second_level(1, 1))
         res = [held("res%d" % i, [P, NP], F32) for i in range(MT)]
         for i in range(MT + 1):
             if i < MT:
-                nc.vector.tensor_tensor(res[i][:], d_sb[i][:].indirect(pos2_sb[:]), cut[i][:], ALU.mult)
+                cut = ring.tile([P, NP], F32, name="cut")
+                nc.scalar.activation(cut[:], e_sb[i][:].indirect(pos1_sb[:]), ACT.Sigmoid, bias=tol_sb[:, i : i + 1])
+                for c in range(CHUNKS):
+                    scores(d_sb, fq, i, c, on_vector if (i < 1 and c == 1) else on_scalar)
+                nc.vector.tensor_tensor(res[i][:], d_sb[i][:].indirect(pos2_sb[:]), cut[:], ALU.mult)
             if i > 0:
                 nc.vector.tensor_tensor(res[i - 1][:], res[i - 1][:], lean_sb[:, i - 1, :], ALU.add)
                 nc.sync.dma_start(out[(i - 1) * P : i * P, :], res[i - 1][:])

@@ -19,10 +19,15 @@ ALU = mybir.AluOpType
 P = 128
 PACK = 4
 KP = P * PACK
-PASSES = 2
+PASSES = K // KP
+QUADS = 4
+ROWS = 4
+LIST_ROWS = 16
 CH = 512
 CHUNKS = S // CH
 MT = S2 // P
+HALVES = 2
+DEPTH = 3
 
 
 def tile_list_guide_cut_tolerance_kernel(
@@ -34,9 +39,17 @@ def tile_list_guide_cut_tolerance_kernel(
         keep = ctx.enter_context(tc.tile_pool(name="keep", bufs=1))
         ring = ctx.enter_context(tc.tile_pool(name="ring", bufs=2))
         psum = ctx.enter_context(tc.psum_pool(name="psum", bufs=8))
+        on_scalar, on_vector = nc.scalar.copy, nc.vector.tensor_copy
 
         def held(name, shape, dtype):
             return keep.tile(shape, dtype, name=name, align_bytes=64)
+
+        def bank():
+            return psum.tile([P, CH], F32, name="bank")
+
+        def grouped_tile():
+            return ring.tile([P, KP * PACK], BF16, name="grouped", bufs=DEPTH, align_bytes=64)
+
 
         def load_list(name, src):
             dst = held(name, list(src.shape), U16)
@@ -49,8 +62,10 @@ def tile_list_guide_cut_tolerance_kernel(
             return dst
 
         def load_table_scales(dst, src):
-            for q in range(4):
-                nc.sync.dma_start(dst[32 * q : 32 * q + 4 * PASSES, :].bitcast(I32), src[:, 4 * q : 4 * q + 4, :].bitcast(I32))
+            for u in range(QUADS):
+                nc.sync.dma_start(
+                    dst[32 * u : 32 * u + ROWS * PASSES, :].bitcast(I32), src[:, ROWS * u : ROWS * (u + 1), :].bitcast(I32)
+                )
 
         def load_w1(a, b):
             dst = held("w1_raw%d%d" % (a, b), [P, PACK, KP], F32)
@@ -70,17 +85,16 @@ def tile_list_guide_cut_tolerance_kernel(
         nc.vector.memset(w4_sc_raw[:].bitcast(I32), 0)
         nc.gpsimd.memset(tab2_sc[:].bitcast(I32), 0)
 
-        w1_raw = {}
-        tab_w, tab2_w = {}, {}
+        w1_raw, tab_w, tab2_w = {}, {}, {}
         offs_sb = load_list("offs_sb", offs)
         b1_sb = load_channel_vector("b1_sb", b1)
         load_table_scales(tab_sc, tab_scales)
         tab_w[0] = load_words("tab_w0", tab_words[0])
         w1_raw[0, 0] = load_w1(0, 0)
-        for q in range(4):
+        for u in range(QUADS):
             nc.sync.dma_start(
-                w4_sc_raw[32 * q : 32 * q + 4, :].bitcast(I32).rearrange("r (a n) -> r a n", a=PASSES),
-                w4_scales[:, 4 * q : 4 * q + 4, :].bitcast(I32).rearrange("a r n -> r a n"),
+                w4_sc_raw[32 * u : 32 * u + ROWS, :].bitcast(I32).rearrange("r (a n) -> r a n", a=PASSES),
+                w4_scales[:, ROWS * u : ROWS * (u + 1), :].bitcast(I32).rearrange("a r n -> r a n"),
             )
         tab_w[1] = load_words("tab_w1", tab_words[1])
         w1_raw[1, 0] = load_w1(1, 0)
@@ -97,10 +111,11 @@ def tile_list_guide_cut_tolerance_kernel(
         pos1_sb = load_list("pos1_sb", pos1)
         pos2_sb = load_list("pos2_sb", pos2)
         tol_sb = held("tol_sb", [P, MT], F32)
-        with nc.allow_non_contiguous_dma(reason="one tolerance for each partition and row tile"):
+        with nc.allow_non_contiguous_dma(reason="guide 128 i + p's tolerance goes to partition p, column i"):
             nc.sync.dma_start(tol_sb[:], tol.rearrange("(i p) -> p i", p=P))
         lean_sb = held("lean_sb", [P, MT, NP], F32)
         nc.sync.dma_start(lean_sb[:], lean.rearrange("(i p) n -> p i n", p=P))
+
 
         def gather(name, window, offsets, count, dtype):
             dst = held(name, [P, count], dtype)
@@ -110,176 +125,178 @@ def tile_list_guide_cut_tolerance_kernel(
         def quantize(name, grouped):
             codes = held(name + "_codes", [P, KP], U32)
             scales = held(name + "_scales", [P, KP], U8)
-            for half in range(2):
-                cols = slice(half * KP // 2, (half + 1) * KP // 2)
+            for half in range(HALVES):
+                cols = slice(half * KP // HALVES, (half + 1) * KP // HALVES)
                 nc.vector.quantize_mx(
                     out=codes[:, cols].bitcast(FP8X4), scales=scales[:, cols], in_=grouped[:, PACK * cols.start : PACK * cols.stop]
                 )
             return codes, scales
 
-        def grouped_tile():
-            return ring.tile([P, KP * PACK], BF16, name="grouped", bufs=3, align_bytes=64)
+        def column_groups(grouped, by_slot, run):
+            dst = grouped[:].rearrange("p (g i t) -> p g t i", i=run, t=PACK)
+            src = by_slot[:].rearrange("p t (g i) -> p g t i", i=run)
+            count = CH // run // HALVES
+            return [(dst[:, half * count : (half + 1) * count], src[:, half * count : (half + 1) * count]) for half in range(HALVES)]
+
+
+        w1q, hq, fq, v_w = {}, {}, {}, {}
 
         def round_w1(a, b, copies):
             grouped = grouped_tile()
             src = w1_raw[a, b][:].rearrange("p j (m t) -> p m j t", t=PACK)
             dst = grouped[:].rearrange("p (t m j) -> p m j t", t=PACK, j=PACK)
             for half, copy in enumerate(copies):
-                copy(dst[:, :, :, 2 * half : 2 * half + 2], src[:, :, :, 2 * half : 2 * half + 2])
+                slots = slice(half * PACK // HALVES, (half + 1) * PACK // HALVES)
+                copy(dst[:, :, :, slots], src[:, :, :, slots])
             return grouped
-
-        on_scalar, on_vector = nc.scalar.copy, nc.vector.tensor_copy
-
-        def bank():
-            return psum.tile([P, CH], F32, name="bank")
-
-        v_sc = gather("v_sc", tab_sc[:], offs_sb[:], S, U8)
-        v_w = {}
-
-        def gather_sites(a, c):
-            v_w[a, c] = gather("v_w%d%d" % (a, c), tab_w[a][:].bitcast(U32), offs_sb[:, c * CH // 16 : (c + 1) * CH // 16], CH, U32)
-
-        w1q, hq, fq = {}, {}, {}
 
         def first_pass(acc, a, b, c, t):
             codes, scales = w1q[a, b]
-            cols = slice(c * CH, (c + 1) * CH)
             nc.tensor.matmul_mx(
                 out=acc[:], lhsT=codes[:, t * P : (t + 1) * P].bitcast(FP8X4), lhsT_scale=scales[:, t * P : (t + 1) * P],
-                rhs=v_w[a, c][:].bitcast(FP8X4), rhs_scale=v_sc[4 * a :, cols], start=(a == 0), stop=(a == PASSES - 1),
+                rhs=v_w[a, c][:].bitcast(FP8X4), rhs_scale=v_sc[ROWS * a :, c * CH : (c + 1) * CH],
+                start=(a == 0), stop=(a == PASSES - 1),
             )
 
-        def tanh_unit(b, accs):
-            th = ring.tile([P, PACK, CH], F32, name="th", bufs=3)
+        def tanh_of(b, accs):
+            th = ring.tile([P, PACK, CH], F32, name="th", bufs=DEPTH)
             for t in range(PACK):
                 nc.scalar.activation(th[:, t, :], accs[t][:], ACT.Tanh, bias=b1_sb[:, PACK * b + t : PACK * b + t + 1])
             return th
-
-        def gain_unit(b, th):
-            grouped = grouped_tile()
-            factor = gain_sb[:, PACK * b : PACK * (b + 1)].unsqueeze(1).unsqueeze(3).to_broadcast([P, CH // 8, PACK, 4])
-            dst = grouped[:].rearrange("p (g i t) -> p g t i", i=4, t=PACK)
-            src = th[:].rearrange("p t (g i) -> p g t i", i=4)
-            for half in range(2):
-                groups = slice(half * CH // 8, (half + 1) * CH // 8)
-                nc.vector.tensor_tensor(dst[:, groups], src[:, groups], factor, ALU.mult)
-            return grouped
 
         def first_level(b, c):
             accs = [bank() for t in range(PACK)]
             for t in range(PACK):
                 for a in range(PASSES):
                     first_pass(accs[t], a, b, c, t)
-            return tanh_unit(b, accs)
+            return tanh_of(b, accs)
 
+        def with_gain(b, th):
+            run = 2
+            grouped = grouped_tile()
+            factor = gain_sb[:, PACK * b : PACK * (b + 1)].unsqueeze(1).unsqueeze(3).to_broadcast([P, CH // run // HALVES, PACK, run])
+            for dst, src in column_groups(grouped, th, run):
+                nc.vector.tensor_tensor(dst, src, factor, ALU.mult)
+            return grouped
+
+        v_sc = gather("v_sc", tab_sc[:], offs_sb[:], S, U8)
         for a in range(PASSES):
             for c in range(CHUNKS):
-                gather_sites(a, c)
+                entries = offs_sb[:, c * CH // LIST_ROWS : (c + 1) * CH // LIST_ROWS]
+                v_w[a, c] = gather("v_w%d%d" % (a, c), tab_w[a][:].bitcast(U32), entries, CH, U32)
+
         w1q[0, 0] = quantize("w1q00", round_w1(0, 0, (on_scalar, on_scalar)))
-        head = [[bank() for t in range(PACK)] for c in range(CHUNKS)]
+        first_banks = [[bank() for t in range(PACK)] for c in range(CHUNKS)]
         for c in range(CHUNKS):
             for t in range(PACK):
-                first_pass(head[c][t], 0, 0, c, t)
+                first_pass(first_banks[c][t], 0, 0, c, t)
         w1q[1, 0] = quantize("w1q10", round_w1(1, 0, (on_vector, on_scalar)))
         for c in range(CHUNKS):
             for t in range(PACK):
-                first_pass(head[c][t], 1, 0, c, t)
+                first_pass(first_banks[c][t], 1, 0, c, t)
         w4_sc = held("w4_sc", [P, PASSES * H], U8)
         nc.vector.tensor_copy(
             w4_sc[:].rearrange("p (g t m) -> p g t m", t=PACK, m=P), w4_sc_raw[:].rearrange("p (g m t) -> p g t m", t=PACK, m=P)
         )
-        th00 = tanh_unit(0, head[0])
+        th00 = tanh_of(0, first_banks[0])
         w1q[0, 1] = quantize("w1q01", round_w1(0, 1, (on_vector, on_vector)))
         w1q[1, 1] = quantize("w1q11", round_w1(1, 1, (on_vector, on_scalar)))
-        hq[0, 0] = quantize("hq00", gain_unit(0, th00))
+
+        hq[0, 0] = quantize("hq00", with_gain(0, th00))
         th10 = first_level(1, 0)
-        hq[1, 0] = quantize("hq10", gain_unit(1, th10))
-        th01 = tanh_unit(0, head[1])
+        hq[1, 0] = quantize("hq10", with_gain(1, th10))
+        th01 = tanh_of(0, first_banks[1])
         w4_w = held("w4_w", [P, PASSES * H], U16)
-        for g in (0, 2, 1, 3):
-            nc.scalar.copy(
-                w4_w[:, g * KP : (g + 1) * KP].rearrange("p (t m) -> p t m", t=PACK),
-                w4_raw[:].bitcast(U16)[:, g * KP : (g + 1) * KP].rearrange("p (m t) -> p t m", t=PACK),
-            )
+        for b in range(PASSES):
+            for a in range(PASSES):
+                cols = slice(a * H + b * KP, a * H + (b + 1) * KP)
+                nc.scalar.copy(
+                    w4_w[:, cols].rearrange("p (t m) -> p t m", t=PACK),
+                    w4_raw[:].bitcast(U16)[:, cols].rearrange("p (m t) -> p t m", t=PACK),
+                )
         v2_w = [gather("v2_w%d" % a, tab2_w[a][:].bitcast(U32), offs2_sb[:], S2, U32) for a in range(PASSES)]
         v2_sc = gather("v2_sc", tab2_sc[:], offs2_sb[:], S2, U8)
         th11 = first_level(1, 1)
-        hq[0, 1] = quantize("hq01", gain_unit(0, th01))
-        hq[1, 1] = quantize("hq11", gain_unit(1, th11))
+        hq[0, 1] = quantize("hq01", with_gain(0, th01))
+        hq[1, 1] = quantize("hq11", with_gain(1, th11))
+
 
         w4_bytes = w4_w[:].bitcast(U8)
 
-        def second_level(b, c):
+        def second_sum(acc, b, c, t, cols):
+            for a in range(PASSES):
+                first = a * H + b * KP + t * P
+                codes, scales = hq[a, c]
+                nc.tensor.matmul_mx(
+                    out=acc, lhsT=w4_bytes[:, 2 * first : 2 * (first + P)].bitcast(FP4X4), lhsT_scale=w4_sc[:, first : first + P],
+                    rhs=codes[:, cols].bitcast(FP8X4), rhs_scale=scales[:, cols], start=(a == 0), stop=(a == PASSES - 1),
+                )
+
+        def second_level_by_scalar(b, c):
+            by_slot = ring.tile([P, PACK, CH], BF16, name="by_slot")
+            for t in range(PACK):
+                acc = bank()
+                second_sum(acc[:], b, c, t, slice(0, CH))
+                nc.scalar.activation(by_slot[:, t, :], acc[:], ACT.Identity, bias=b2_sb[:, PACK * b + t : PACK * b + t + 1])
+            run = 4
+            grouped = grouped_tile()
+            for dst, src in column_groups(grouped, by_slot, run):
+                nc.vector.tensor_copy(dst, src)
+            return grouped
+
+        def second_level_by_vector(b, c):
             grouped = grouped_tile()
             shift = b2_sb[:, PACK * b : PACK * (b + 1)].unsqueeze(1).to_broadcast([P, P, PACK])
-            for q in range(CH // P):
+            for quarter in range(CH // P):
                 acc = bank()
-                cols = slice(q * P, (q + 1) * P)
                 for t in range(PACK):
-                    for a in range(PASSES):
-                        first = a * H + b * KP + t * P
-                        codes, scales = hq[a, c]
-                        nc.tensor.matmul_mx(
-                            out=acc[:, t * P : (t + 1) * P],
-                            lhsT=w4_bytes[:, 2 * first : 2 * (first + P)].bitcast(FP4X4), lhsT_scale=w4_sc[:, first : first + P],
-                            rhs=codes[:, cols].bitcast(FP8X4), rhs_scale=scales[:, cols], start=(a == 0), stop=(a == PASSES - 1),
-                        )
+                    second_sum(acc[:, t * P : (t + 1) * P], b, c, t, slice(quarter * P, (quarter + 1) * P))
                 nc.vector.tensor_tensor(
-                    grouped[:, q * KP : (q + 1) * KP].rearrange("p (n t) -> p n t", t=PACK),
+                    grouped[:, quarter * KP : (quarter + 1) * KP].rearrange("p (n t) -> p n t", t=PACK),
                     acc[:].rearrange("p (t n) -> p n t", t=PACK), shift, ALU.add,
                 )
             return grouped
 
-        def second_level_wide(b, c):
-            planes = ring.tile([P, PACK, CH], BF16, name="planes")
-            for t in range(PACK):
-                acc = bank()
-                for a in range(PASSES):
-                    first = a * H + b * KP + t * P
-                    codes, scales = hq[a, c]
-                    nc.tensor.matmul_mx(
-                        out=acc[:], lhsT=w4_bytes[:, 2 * first : 2 * (first + P)].bitcast(FP4X4), lhsT_scale=w4_sc[:, first : first + P],
-                        rhs=codes[:].bitcast(FP8X4), rhs_scale=scales[:], start=(a == 0), stop=(a == PASSES - 1),
-                    )
-                nc.scalar.activation(planes[:, t, :], acc[:], ACT.Identity, bias=b2_sb[:, PACK * b + t : PACK * b + t + 1])
-            grouped = grouped_tile()
-            dst = grouped[:].rearrange("p (g i t) -> p g t i", i=4, t=PACK)
-            src = planes[:].rearrange("p t (g i) -> p g t i", i=4)
-            for half in range(2):
-                groups = slice(half * CH // 8, (half + 1) * CH // 8)
-                nc.vector.tensor_copy(dst[:, groups], src[:, groups])
-            return grouped
 
         e_sb = [held("e_sb%d" % i, [P, S], F32) for i in range(MT)]
         d_sb = [held("d_sb%d" % i, [P, S], F32) for i in range(MT)]
 
-        def scores(dst, level, i, c, copy=on_scalar):
-            acc = bank()
+        def scores(dst, level, i, c, copy=on_scalar, pieces=1):
             rows = slice(i * P, (i + 1) * P)
-            for a in range(PASSES):
-                codes, scales = level[a, c]
-                nc.tensor.matmul_mx(
-                    out=acc[:], lhsT=v2_w[a][:, rows].bitcast(FP8X4), lhsT_scale=v2_sc[4 * a :, rows],
-                    rhs=codes[:].bitcast(FP8X4), rhs_scale=scales[:], start=(a == 0), stop=(a == PASSES - 1),
-                )
-            copy(dst[i][:, c * CH : (c + 1) * CH], acc[:])
+            width = CH // pieces
+            for piece in range(pieces):
+                acc = bank()
+                cols = slice(piece * width, (piece + 1) * width)
+                for a in range(PASSES):
+                    codes, scales = level[a, c]
+                    nc.tensor.matmul_mx(
+                        out=acc[:, :width], lhsT=v2_w[a][:, rows].bitcast(FP8X4), lhsT_scale=v2_sc[ROWS * a :, rows],
+                        rhs=codes[:, cols].bitcast(FP8X4), rhs_scale=scales[:, cols], start=(a == 0), stop=(a == PASSES - 1),
+                    )
+                copy(dst[i][:, c * CH + cols.start : c * CH + cols.stop], acc[:, :width])
 
         for b in range(PASSES):
-            fq[b, 0] = quantize("fq%d0" % b, second_level_wide(b, 0))
-        for i in range(MT):
-            scores(e_sb, hq, i, 0)
-        fq[0, 1] = quantize("fq01", second_level(0, 1))
-        for i in range(MT):
-            scores(e_sb, hq, i, 1)
-        fq[1, 1] = quantize("fq11", second_level(1, 1))
+            fq[b, 0] = quantize("fq%d0" % b, second_level_by_scalar(b, 0))
+        for c in range(CHUNKS):
+            for i in range(MT):
+                scores(e_sb, hq, i, c)
+        for b in range(PASSES):
+            fq[b, 1] = quantize("fq%d1" % b, second_level_by_vector(b, 1))
+
         res = [held("res%d" % i, [P, NP], F32) for i in range(MT)]
         for i in range(MT + 1):
             if i < MT:
-                cut = ring.tile([P, NP], F32, name="cut")
+                cut = ring.tile([P, NP], F32, name="cut", bufs=DEPTH)
                 nc.scalar.activation(cut[:], e_sb[i][:].indirect(pos1_sb[:]), ACT.Sigmoid, bias=tol_sb[:, i : i + 1])
                 for c in range(CHUNKS):
-                    scores(d_sb, fq, i, c, on_vector if (i < 1 and c == 1) else on_scalar)
+                    if (i, c) == (0, CHUNKS - 1):
+                        scores(d_sb, fq, i, c, on_vector, pieces=HALVES)
+                    else:
+                        scores(d_sb, fq, i, c)
                 nc.vector.tensor_tensor(res[i][:], d_sb[i][:].indirect(pos2_sb[:]), cut[:], ALU.mult)
             if i > 0:
-                nc.vector.tensor_tensor(res[i - 1][:], res[i - 1][:], lean_sb[:, i - 1, :], ALU.add)
-                nc.sync.dma_start(out[(i - 1) * P : i * P, :], res[i - 1][:])
+                pieces = HALVES if i == MT else 1
+                for piece in range(pieces):
+                    cols = slice(piece * NP // pieces, (piece + 1) * NP // pieces)
+                    nc.vector.tensor_tensor(res[i - 1][:, cols], res[i - 1][:, cols], lean_sb[:, i - 1, cols], ALU.add)
+                    nc.sync.dma_start(out[(i - 1) * P : i * P, cols], res[i - 1][:, cols])

from contextlib import ExitStack

import concourse.mybir as mybir

K, H, T, S, S2, NP = 1024, 1024, 2048, 1024, 512, 512
FLOPS = 2 * (K * H * S + H * H * S + 2 * H * S2 * S)

F32 = mybir.dt.float32
BF16 = mybir.dt.bfloat16
I32 = mybir.dt.int32
U32 = mybir.dt.uint32
U16 = mybir.dt.uint16
U8 = mybir.dt.uint8
FP8X4 = mybir.dt.float8_e4m3fn_x4
FP4X4 = mybir.dt.float4_e2m1fn_x4
ACT = mybir.ActivationFunctionType
ALU = mybir.AluOpType

P = 128
PACK = 4
KP = P * PACK
PASSES = K // KP
QUADS = 4
ROWS = 4
LIST_ROWS = 16
CH = 512
CHUNKS = S // CH
MT = S2 // P
HALVES = 2
DEPTH = 3


def tile_list_guide_cut_tolerance_kernel(
    tc, tab_words, tab_scales, offs, tab2_words, tab2_scales, offs2, pos1, pos2,
    w1, b1, gain, w4_words, w4_scales, b2, tol, lean, out,
):
    nc = tc.nc
    with ExitStack() as ctx:
        keep = ctx.enter_context(tc.tile_pool(name="keep", bufs=1))
        ring = ctx.enter_context(tc.tile_pool(name="ring", bufs=2))
        psum = ctx.enter_context(tc.psum_pool(name="psum", bufs=8))
        on_scalar, on_vector = nc.scalar.copy, nc.vector.tensor_copy

        def held(name, shape, dtype):
            return keep.tile(shape, dtype, name=name, align_bytes=64)

        def bank():
            return psum.tile([P, CH], F32, name="bank")

        def grouped_tile():
            return ring.tile([P, KP * PACK], BF16, name="grouped", bufs=DEPTH, align_bytes=64)


        def load_list(name, src):
            dst = held(name, list(src.shape), U16)
            nc.sync.dma_start(dst[:], src)
            return dst

        def load_words(name, src):
            dst = held(name, [P, T], I32)
            nc.sync.dma_start(dst[:], src.rearrange("p t i -> p (t i)").bitcast(I32))
            return dst

        def load_table_scales(dst, src):
            for u in range(QUADS):
                nc.sync.dma_start(
                    dst[32 * u : 32 * u + ROWS * PASSES, :].bitcast(I32), src[:, ROWS * u : ROWS * (u + 1), :].bitcast(I32)
                )

        def load_w1(a, b):
            dst = held("w1_raw%d%d" % (a, b), [P, PACK, KP], F32)
            nc.sync.dma_start(dst[:], w1[a * KP : (a + 1) * KP, b * KP : (b + 1) * KP].rearrange("(p j) c -> p j c", j=PACK))
            return dst

        def load_channel_vector(name, src):
            dst = held(name, [P, PASSES * PACK], F32)
            nc.sync.dma_start(dst[:].rearrange("p (b t) -> p b t", t=PACK), src.rearrange("(b p t) -> p b t", p=P, t=PACK))
            return dst

        tab_sc = held("tab_sc", [P, T], U8)
        tab2_sc = held("tab2_sc", [P, T], U8)
        w4_sc_raw = held("w4_sc_raw", [P, PASSES * H], U8)
        nc.gpsimd.memset(tab_sc[:, : T // 2].bitcast(I32), 0)
        nc.vector.memset(tab_sc[:, T // 2 :].bitcast(I32), 0)
        nc.vector.memset(w4_sc_raw[:].bitcast(I32), 0)
        nc.gpsimd.memset(tab2_sc[:].bitcast(I32), 0)

        w1_raw, tab_w, tab2_w = {}, {}, {}
        offs_sb = load_list("offs_sb", offs)
        b1_sb = load_channel_vector("b1_sb", b1)
        load_table_scales(tab_sc, tab_scales)
        tab_w[0] = load_words("tab_w0", tab_words[0])
        w1_raw[0, 0] = load_w1(0, 0)
        for u in range(QUADS):
            nc.sync.dma_start(
                w4_sc_raw[32 * u : 32 * u + ROWS, :].bitcast(I32).rearrange("r (a n) -> r a n", a=PASSES),
                w4_scales[:, ROWS * u : ROWS * (u + 1), :].bitcast(I32).rearrange("a r n -> r a n"),
            )
        tab_w[1] = load_words("tab_w1", tab_words[1])
        w1_raw[1, 0] = load_w1(1, 0)
        w1_raw[0, 1] = load_w1(0, 1)
        w1_raw[1, 1] = load_w1(1, 1)
        gain_sb = load_channel_vector("gain_sb", gain)
        w4_raw = held("w4_raw", [P, PASSES * H // 2], I32)
        nc.sync.dma_start(w4_raw[:].rearrange("p (a n) -> p a n", a=PASSES), w4_words.bitcast(I32).rearrange("a p n -> p a n"))
        offs2_sb = load_list("offs2_sb", offs2)
        tab2_w[0] = load_words("tab2_w0", tab2_words[0])
        load_table_scales(tab2_sc, tab2_scales)
        tab2_w[1] = load_words("tab2_w1", tab2_words[1])
        b2_sb = load_channel_vector("b2_sb", b2)
        pos1_sb = load_list("pos1_sb", pos1)
        pos2_sb = load_list("pos2_sb", pos2)
        tol_sb = held("tol_sb", [P, MT], F32)
        with nc.allow_non_contiguous_dma(reason="guide 128 i + p's tolerance goes to partition p, column i"):
            nc.sync.dma_start(tol_sb[:], tol.rearrange("(i p) -> p i", p=P))
        lean_sb = held("lean_sb", [P, MT, NP], F32)
        nc.sync.dma_start(lean_sb[:], lean.rearrange("(i p) n -> p i n", p=P))


        def gather(name, window, offsets, count, dtype):
            dst = held(name, [P, count], dtype)
            nc.vector.tensor_copy(dst[:], window.indirect(offsets))
            return dst

        def quantize(name, grouped):
            codes = held(name + "_codes", [P, KP], U32)
            scales = held(name + "_scales", [P, KP], U8)
            for half in range(HALVES):
                cols = slice(half * KP // HALVES, (half + 1) * KP // HALVES)
                nc.vector.quantize_mx(
                    out=codes[:, cols].bitcast(FP8X4), scales=scales[:, cols], in_=grouped[:, PACK * cols.start : PACK * cols.stop]
                )
            return codes, scales

        def column_groups(grouped, by_slot, run):
            dst = grouped[:].rearrange("p (g i t) -> p g t i", i=run, t=PACK)
            src = by_slot[:].rearrange("p t (g i) -> p g t i", i=run)
            count = CH // run // HALVES
            return [(dst[:, half * count : (half + 1) * count], src[:, half * count : (half + 1) * count]) for half in range(HALVES)]


        w1q, hq, fq, v_w = {}, {}, {}, {}

        def round_w1(a, b, copies):
            grouped = grouped_tile()
            src = w1_raw[a, b][:].rearrange("p j (m t) -> p m j t", t=PACK)
            dst = grouped[:].rearrange("p (t m j) -> p m j t", t=PACK, j=PACK)
            for half, copy in enumerate(copies):
                slots = slice(half * PACK // HALVES, (half + 1) * PACK // HALVES)
                copy(dst[:, :, :, slots], src[:, :, :, slots])
            return grouped

        def first_pass(acc, a, b, c, t):
            codes, scales = w1q[a, b]
            nc.tensor.matmul_mx(
                out=acc[:], lhsT=codes[:, t * P : (t + 1) * P].bitcast(FP8X4), lhsT_scale=scales[:, t * P : (t + 1) * P],
                rhs=v_w[a, c][:].bitcast(FP8X4), rhs_scale=v_sc[ROWS * a :, c * CH : (c + 1) * CH],
                start=(a == 0), stop=(a == PASSES - 1),
            )

        def tanh_of(b, accs):
            th = ring.tile([P, PACK, CH], F32, name="th", bufs=DEPTH)
            for t in range(PACK):
                nc.scalar.activation(th[:, t, :], accs[t][:], ACT.Tanh, bias=b1_sb[:, PACK * b + t : PACK * b + t + 1])
            return th

        def first_level(b, c):
            accs = [bank() for t in range(PACK)]
            for t in range(PACK):
                for a in range(PASSES):
                    first_pass(accs[t], a, b, c, t)
            return tanh_of(b, accs)

        def with_gain(b, th):
            run = 2
            grouped = grouped_tile()
            factor = gain_sb[:, PACK * b : PACK * (b + 1)].unsqueeze(1).unsqueeze(3).to_broadcast([P, CH // run // HALVES, PACK, run])
            for dst, src in column_groups(grouped, th, run):
                nc.vector.tensor_tensor(dst, src, factor, ALU.mult)
            return grouped

        v_sc = gather("v_sc", tab_sc[:], offs_sb[:], S, U8)
        for a in range(PASSES):
            for c in range(CHUNKS):
                entries = offs_sb[:, c * CH // LIST_ROWS : (c + 1) * CH // LIST_ROWS]
                v_w[a, c] = gather("v_w%d%d" % (a, c), tab_w[a][:].bitcast(U32), entries, CH, U32)

        w1q[0, 0] = quantize("w1q00", round_w1(0, 0, (on_scalar, on_scalar)))
        first_banks = [[bank() for t in range(PACK)] for c in range(CHUNKS)]
        for c in range(CHUNKS):
            for t in range(PACK):
                first_pass(first_banks[c][t], 0, 0, c, t)
        w1q[1, 0] = quantize("w1q10", round_w1(1, 0, (on_vector, on_scalar)))
        for c in range(CHUNKS):
            for t in range(PACK):
                first_pass(first_banks[c][t], 1, 0, c, t)
        w4_sc = held("w4_sc", [P, PASSES * H], U8)
        nc.vector.tensor_copy(
            w4_sc[:].rearrange("p (g t m) -> p g t m", t=PACK, m=P), w4_sc_raw[:].rearrange("p (g m t) -> p g t m", t=PACK, m=P)
        )
        th00 = tanh_of(0, first_banks[0])
        w1q[0, 1] = quantize("w1q01", round_w1(0, 1, (on_vector, on_vector)))
        w1q[1, 1] = quantize("w1q11", round_w1(1, 1, (on_vector, on_scalar)))

        hq[0, 0] = quantize("hq00", with_gain(0, th00))
        th10 = first_level(1, 0)
        hq[1, 0] = quantize("hq10", with_gain(1, th10))
        th01 = tanh_of(0, first_banks[1])
        w4_w = held("w4_w", [P, PASSES * H], U16)
        for b in range(PASSES):
            for a in range(PASSES):
                cols = slice(a * H + b * KP, a * H + (b + 1) * KP)
                nc.scalar.copy(
                    w4_w[:, cols].rearrange("p (t m) -> p t m", t=PACK),
                    w4_raw[:].bitcast(U16)[:, cols].rearrange("p (m t) -> p t m", t=PACK),
                )
        v2_w = [gather("v2_w%d" % a, tab2_w[a][:].bitcast(U32), offs2_sb[:], S2, U32) for a in range(PASSES)]
        v2_sc = gather("v2_sc", tab2_sc[:], offs2_sb[:], S2, U8)
        th11 = first_level(1, 1)
        hq[0, 1] = quantize("hq01", with_gain(0, th01))
        hq[1, 1] = quantize("hq11", with_gain(1, th11))


        w4_bytes = w4_w[:].bitcast(U8)

        def second_sum(acc, b, c, t, cols):
            for a in range(PASSES):
                first = a * H + b * KP + t * P
                codes, scales = hq[a, c]
                nc.tensor.matmul_mx(
                    out=acc, lhsT=w4_bytes[:, 2 * first : 2 * (first + P)].bitcast(FP4X4), lhsT_scale=w4_sc[:, first : first + P],
                    rhs=codes[:, cols].bitcast(FP8X4), rhs_scale=scales[:, cols], start=(a == 0), stop=(a == PASSES - 1),
                )

        def second_level_by_scalar(b, c):
            by_slot = ring.tile([P, PACK, CH], BF16, name="by_slot")
            for t in range(PACK):
                acc = bank()
                second_sum(acc[:], b, c, t, slice(0, CH))
                nc.scalar.activation(by_slot[:, t, :], acc[:], ACT.Identity, bias=b2_sb[:, PACK * b + t : PACK * b + t + 1])
            run = 4
            grouped = grouped_tile()
            for dst, src in column_groups(grouped, by_slot, run):
                nc.vector.tensor_copy(dst, src)
            return grouped

        def second_level_by_vector(b, c):
            grouped = grouped_tile()
            shift = b2_sb[:, PACK * b : PACK * (b + 1)].unsqueeze(1).to_broadcast([P, P, PACK])
            for quarter in range(CH // P):
                acc = bank()
                for t in range(PACK):
                    second_sum(acc[:, t * P : (t + 1) * P], b, c, t, slice(quarter * P, (quarter + 1) * P))
                nc.vector.tensor_tensor(
                    grouped[:, quarter * KP : (quarter + 1) * KP].rearrange("p (n t) -> p n t", t=PACK),
                    acc[:].rearrange("p (t n) -> p n t", t=PACK), shift, ALU.add,
                )
            return grouped


        e_sb = [held("e_sb%d" % i, [P, S], F32) for i in range(MT)]
        d_sb = [held("d_sb%d" % i, [P, S], F32) for i in range(MT)]

        def scores(dst, level, i, c, copy=on_scalar, pieces=1):
            rows = slice(i * P, (i + 1) * P)
            width = CH // pieces
            for piece in range(pieces):
                acc = bank()
                cols = slice(piece * width, (piece + 1) * width)
                for a in range(PASSES):
                    codes, scales = level[a, c]
                    nc.tensor.matmul_mx(
                        out=acc[:, :width], lhsT=v2_w[a][:, rows].bitcast(FP8X4), lhsT_scale=v2_sc[ROWS * a :, rows],
                        rhs=codes[:, cols].bitcast(FP8X4), rhs_scale=scales[:, cols], start=(a == 0), stop=(a == PASSES - 1),
                    )
                copy(dst[i][:, c * CH + cols.start : c * CH + cols.stop], acc[:, :width])

        for b in range(PASSES):
            fq[b, 0] = quantize("fq%d0" % b, second_level_by_scalar(b, 0))
        for c in range(CHUNKS):
            for i in range(MT):
                scores(e_sb, hq, i, c)
        for b in range(PASSES):
            fq[b, 1] = quantize("fq%d1" % b, second_level_by_vector(b, 1))

        res = [held("res%d" % i, [P, NP], F32) for i in range(MT)]
        for i in range(MT + 1):
            if i < MT:
                cut = ring.tile([P, NP], F32, name="cut", bufs=DEPTH)
                nc.scalar.activation(cut[:], e_sb[i][:].indirect(pos1_sb[:]), ACT.Sigmoid, bias=tol_sb[:, i : i + 1])
                for c in range(CHUNKS):
                    if (i, c) == (0, CHUNKS - 1):
                        scores(d_sb, fq, i, c, on_vector, pieces=HALVES)
                    else:
                        scores(d_sb, fq, i, c)
                nc.vector.tensor_tensor(res[i][:], d_sb[i][:].indirect(pos2_sb[:]), cut[:], ALU.mult)
            if i > 0:
                pieces = HALVES if i == MT else 1
                for piece in range(pieces):
                    cols = slice(piece * NP // pieces, (piece + 1) * NP // pieces)
                    nc.vector.tensor_tensor(res[i - 1][:, cols], res[i - 1][:, cols], lean_sb[:, i - 1, cols], ALU.add)
                    nc.sync.dma_start(out[(i - 1) * P : i * P, cols], res[i - 1][:, cols])
